import numpy as np
import ml_dtypes


def mxq(x, axis, fmt="e4m3"):
    dtype, down = {"e4m3": (ml_dtypes.float8_e4m3fn, 7), "e5m2": (ml_dtypes.float8_e5m2, 14)}[fmt]
    v = np.moveaxis(np.asarray(x, np.float32).astype(ml_dtypes.bfloat16).astype(np.float64), axis, -1)
    blocks = v.reshape(v.shape[:-1] + (-1, 32))
    amax = np.abs(blocks).max(-1, keepdims=True)
    byte = np.maximum(np.where(amax > 0, np.frexp(amax)[1] - 1 + 127, 0) - down, 1)
    scale = np.exp2(byte - 127.0)
    codes = (blocks / scale).astype(np.float32).astype(dtype).astype(np.float64)
    return np.moveaxis((codes * scale).reshape(v.shape), -1, axis)


WIDE = False


def mx_kscale(k):
    if not WIDE:
        return np.ones(k)
    levels = np.array([10, -10, 5, -5, 0])
    if k % 512:
        return np.exp2(np.random.permutation(np.resize(levels, k // 32))).repeat(32)
    a = np.empty((k // 512, 16))
    for p in range(k // 512):
        a[p, :8] = np.random.permutation(np.resize(levels, 8))
        for g in range(8):
            far = levels[np.abs(levels - a[p, g]) >= 10]
            a[p, g + 8] = far[np.random.randint(len(far))]
    return np.exp2(a.ravel()).repeat(32)


def f64(x):
    return np.asarray(x).astype(np.float64)


def striped(idx):
    return np.tile(idx.reshape(-1, 16).T, (8, 1)).astype(np.uint16)


def unstriped(offs):
    return offs[:16].T.reshape(-1).astype(np.int64)


def relu(v):
    return np.maximum(v, 0.0)


K, T, D, S, V, N = 1024, 2048, 4, 512, 256, 512


def setup_inputs():
    n = np.random.standard_normal
    s = mx_kscale(K)[:, None]
    return {
        "xT": (n((K, T)) * s).astype(np.float32),
        "w": (n((K, N)) / np.sqrt(K) / s).astype(np.float32),
        "b": (0.3 * n((N, 1))).astype(np.float32),
        "gate": np.tile(np.random.uniform(0.2, 1.0, (D, 1, V)) / np.sqrt(D), (1, N, 1)).astype(np.float32),
        "offs": striped(np.random.permutation(T)[:S]),
        "pos1": striped(np.random.permutation(S)[:V]),
        "pos2": striped(np.random.permutation(S)[:V]),
        "pos3": striped(np.random.permutation(S)[:V]),
        "pos4": striped(np.random.permutation(S)[:V]),
    }


def reference(xT, w, b, gate, offs, pos1, pos2, pos3, pos4):
    idx = unstriped(offs)
    xq = mxq(f64(xT)[:, idx], 0, "e4m3")
    y = mxq(f64(w), 0, "e4m3").T @ xq
    y = relu(y + f64(b))
    return sum(f64(gate[d]) * y[:, unstriped(p)] for d, p in enumerate((pos1, pos2, pos3, pos4)))

@@ -1,0 +1,186 @@
+from contextlib import ExitStack
+
+import concourse.mybir as mybir
+from concourse.masks import make_identity
+
+F32 = mybir.dt.float32
+BF16 = mybir.dt.bfloat16
+U32 = mybir.dt.uint32
+U16 = mybir.dt.uint16
+U8 = mybir.dt.uint8
+FP8X4 = mybir.dt.float8_e4m3fn_x4
+MULT = mybir.AluOpType.mult
+ADD = mybir.AluOpType.add
+RELU = mybir.ActivationFunctionType.Relu
+
+K, T, D, S, V, N = 1024, 2048, 4, 512, 256, 512
+P = 128
+PACK = 4
+PASSES = K // (P * PACK)
+BLOCKS = N // P
+HALF = S // 2
+FLOPS = 2 * N * K * S
+
+
+def tile_picked_sub_lin_relu_sub_e_kernel(tc, xT, w, b, gate, offs, pos1, pos2, pos3, pos4, out):
+    nc = tc.nc
+    positions = (pos1, pos2, pos3, pos4)
+    with ExitStack() as ctx:
+        lists = ctx.enter_context(tc.tile_pool(name="lists", bufs=1))
+        keep = ctx.enter_context(tc.tile_pool(name="keep", bufs=1))
+        work = ctx.enter_context(tc.tile_pool(name="work", bufs=2))
+        psum = ctx.enter_context(tc.psum_pool(name="psum", bufs=1))
+
+        xv = xT.rearrange("(a p j) t -> a j p t", a=PASSES, j=PACK)
+        wv = w.rearrange("(a p j) n -> a p j n", a=PASSES, j=PACK)
+
+        offs_sb = lists.tile([P, S // 16], U16, name="offs_sb")
+        pos_sb = [lists.tile([P, V // 16], U16, name=f"pos_sb{d}") for d in range(D)]
+
+        nc.sync.dma_start(offs_sb[:], offs)
+        groups = ((0, 1), (1, 1), (2, 2))
+        w_raw = [keep.tile([P, PASSES, PACK, nb * P], F32, name=f"w_raw{g}") for g, (c0, nb) in enumerate(groups)]
+
+        def load_w(g):
+            c0, nb = groups[g]
+            for a in range(PASSES):
+                nc.sync.dma_start(w_raw[g][:, a, :, :], wv[a][:, :, c0 * P : (c0 + nb) * P])
+
+        gate_sb = [keep.tile([P, D, V], F32, name=f"gate_sb{c}") for c in range(BLOCKS)]
+
+        def load_gate(c):
+            nc.sync.dma_start(gate_sb[c][:], gate[:, c * P : (c + 1) * P, :].rearrange("d p v -> p d v"))
+
+        load_w(0)
+        x_sb = [[keep.tile([P, T], F32, name=f"x_sb{a}{j}") for j in range(PACK)] for a in range(PASSES)]
+        for a in range(PASSES):
+            for j in range(PACK):
+                nc.sync.dma_start(x_sb[a][j][:], xv[a, j])
+        load_gate(0)
+        for d in range(D):
+            nc.sync.dma_start(pos_sb[d][:], positions[d])
+        load_w(1)
+        load_gate(1)
+        load_w(2)
+        load_gate(2)
+        load_gate(3)
+
+        ident = keep.tile([P, P], F32, name="ident")
+        make_identity(nc, ident[:])
+        b_rows = keep.tile([P, P], F32, name="b_rows")
+        nc.vector.memset(b_rows[:], 0.0)
+        nc.scalar.dma_start(b_rows[0:BLOCKS, :], b.rearrange("(c p) o -> c (p o)", c=BLOCKS))
+        b_ps = psum.tile([P, P], F32, name="b_ps")
+        nc.tensor.transpose(b_ps[:], b_rows[:], ident[:])
+        b_cols = keep.tile([P, BLOCKS], F32, name="b_cols")
+        nc.scalar.copy(b_cols[:], b_ps[:, 0:BLOCKS])
+
+        w_grp = [keep.tile([P, PASSES, nb * P, PACK], BF16, name=f"w_grp{g}", align_bytes=64) for g, (c0, nb) in enumerate(groups)]
+        w_codes = [keep.tile([P, PASSES, nb * P], U32, name=f"w_codes{g}", align_bytes=64) for g, (c0, nb) in enumerate(groups)]
+        w_scales = [keep.tile([P, PASSES, nb * P], U8, name=f"w_scales{g}", align_bytes=64) for g, (c0, nb) in enumerate(groups)]
+
+        def interleave_w(g):
+            for a in range(PASSES):
+                nc.scalar.copy(w_grp[g][:, a, :, :], w_raw[g][:, a, :, :].rearrange("p j n -> p n j"))
+
+        def quantize_w(g):
+            nc.vector.quantize_mx(
+                out=w_codes[g][:].rearrange("p a n -> p (a n)").bitcast(FP8X4),
+                scales=w_scales[g][:].rearrange("p a n -> p (a n)"),
+                in_=w_grp[g][:].rearrange("p a n j -> p (a n j)"),
+            )
+
+        x_grp = [keep.tile([P, S, PACK], BF16, name=f"x_grp{a}", align_bytes=64) for a in range(PASSES)]
+        x_codes = [keep.tile([P, S], U32, name=f"x_codes{a}", align_bytes=64) for a in range(PASSES)]
+        x_scales = [keep.tile([P, S], U8, name=f"x_scales{a}", align_bytes=64) for a in range(PASSES)]
+
+        def gather_x(a, j, s0, s1):
+            nc.vector.tensor_copy(x_grp[a][:, s0:s1, j], x_sb[a][j][:].indirect(offs_sb[:, s0 // 16 : s1 // 16]))
+
+        def quantize_x(a, s0, s1):
+            nc.vector.quantize_mx(
+                out=x_codes[a][:, s0:s1].bitcast(FP8X4),
+                scales=x_scales[a][:, s0:s1],
+                in_=x_grp[a][:, s0:s1, :].rearrange("p s j -> p (s j)"),
+            )
+
+        y_sb = [keep.tile([P, S], F32, name=f"y_sb{c}") for c in range(BLOCKS)]
+
+        def multiply(acc, c, a, s0, s1):
+            g = min(c, 2)
+            m0 = (c - groups[g][0]) * P
+            nc.tensor.matmul_mx(
+                out=acc[:],
+                lhsT=w_codes[g][:, a, m0 : m0 + P].bitcast(FP8X4),
+                lhsT_scale=w_scales[g][:, a, m0 : m0 + P],
+                rhs=x_codes[a][:, s0:s1].bitcast(FP8X4),
+                rhs_scale=x_scales[a][:, s0:s1],
+                start=(a == 0),
+                stop=(a == PASSES - 1),
+            )
+
+        def finish(acc, c, s0, s1):
+            nc.scalar.activation(y_sb[c][:, s0:s1], acc[:], RELU, bias=b_cols[:, c : c + 1])
+
+        prods = [[keep.tile([P, V], F32, name=f"prod{c}{d}") for d in range(D)] for c in range(BLOCKS)]
+
+        def neighbour(c, d):
+            nc.vector.tensor_tensor(prods[c][d][:], y_sb[c][:].indirect(pos_sb[d][:]), gate_sb[c][:, d, :], MULT)
+
+        interleave_w(0)
+        quantize_w(0)
+        for j in range(PACK):
+            gather_x(0, j, 0, S)
+        quantize_x(0, 0, S)
+        halves = ((0, HALF), (HALF, S))
+        acc0 = [psum.tile([P, HALF], F32, name=f"acc0{h}") for h in range(2)]
+        for h, (s0, s1) in enumerate(halves):
+            multiply(acc0[h], 0, 0, s0, s1)
+        for j in range(PACK - 1):
+            gather_x(1, j, 0, S)
+        for s0, s1 in halves:
+            gather_x(1, PACK - 1, s0, s1)
+        for h, (s0, s1) in enumerate(halves):
+            quantize_x(1, s0, s1)
+            multiply(acc0[h], 0, 1, s0, s1)
+            finish(acc0[h], 0, s0, s1)
+
+        def later_block(c):
+            acc = psum.tile([P, S], F32, name="acc", bufs=3)
+            for a in range(PASSES):
+                multiply(acc, c, a, 0, S)
+            finish(acc, c, 0, S)
+
+        def sums(c):
+            first = work.tile([P, V], F32, name="first")
+            second = work.tile([P, V], F32, name="second")
+            total = work.tile([P, V], F32, name="total")
+            nc.vector.tensor_tensor(first[:], prods[c][0][:], prods[c][1][:], ADD)
+            nc.vector.tensor_tensor(second[:], prods[c][2][:], prods[c][3][:], ADD)
+            nc.vector.tensor_tensor(total[:], first[:], second[:], ADD)
+            nc.sync.dma_start(out[c * P : (c + 1) * P, :], total[:])
+
+        interleave_w(1)
+        neighbour(0, 0)
+        neighbour(0, 1)
+        quantize_w(1)
+        later_block(1)
+        interleave_w(2)
+        neighbour(0, 2)
+        neighbour(0, 3)
+        neighbour(1, 0)
+        quantize_w(2)
+        later_block(2)
+        later_block(3)
+        sums(0)
+        for d in range(1, D):
+            neighbour(1, d)
+        neighbour(2, 0)
+        sums(1)
+        for d in range(1, D):
+            neighbour(2, d)
+        neighbour(3, 0)
+        sums(2)
+        for d in range(1, D):
+            neighbour(3, d)
+        sums(3)

@@ -33,66 +33,48 @@ def tile_picked_sub_lin_relu_sub_e_kernel(tc, xT, w, b, gate, offs, pos1, pos2, 
 
         xv = xT.rearrange("(a p j) t -> a j p t", a=PASSES, j=PACK)
         wv = w.rearrange("(a p j) n -> a p j n", a=PASSES, j=PACK)
+        gv = gate.rearrange("d (p c) v -> d p c v", c=BLOCKS)
+        ov = out.rearrange("(p c) v -> c p v", c=BLOCKS)
 
         offs_sb = lists.tile([P, S // 16], U16, name="offs_sb")
         pos_sb = [lists.tile([P, V // 16], U16, name=f"pos_sb{d}") for d in range(D)]
+        w_raw = [keep.tile([P, PACK, N], F32, name=f"w_raw{a}") for a in range(PASSES)]
+        x_sb = [[keep.tile([P, T], F32, name=f"x_sb{a}{j}") for j in range(PACK)] for a in range(PASSES)]
+        gate_sb = [keep.tile([P, BLOCKS, V], F32, name=f"gate_sb{d}") for d in range(D)]
+        b_cols = keep.tile([P, BLOCKS], F32, name="b_cols")
 
         nc.sync.dma_start(offs_sb[:], offs)
-        groups = ((0, 1), (1, 1), (2, 2))
-        w_raw = [keep.tile([P, PASSES, PACK, nb * P], F32, name=f"w_raw{g}") for g, (c0, nb) in enumerate(groups)]
-
-        def load_w(g):
-            c0, nb = groups[g]
-            for a in range(PASSES):
-                nc.sync.dma_start(w_raw[g][:, a, :, :], wv[a][:, :, c0 * P : (c0 + nb) * P])
-
-        gate_sb = [keep.tile([P, D, V], F32, name=f"gate_sb{c}") for c in range(BLOCKS)]
-
-        def load_gate(c):
-            nc.sync.dma_start(gate_sb[c][:], gate[:, c * P : (c + 1) * P, :].rearrange("d p v -> p d v"))
-
-        load_w(0)
-        x_sb = [[keep.tile([P, T], F32, name=f"x_sb{a}{j}") for j in range(PACK)] for a in range(PASSES)]
+        for a in range(PASSES):
+            nc.sync.dma_start(w_raw[a][:], wv[a])
+        nc.scalar.dma_start(b_cols[:], b.rearrange("(p c) o -> p (c o)", c=BLOCKS))
         for a in range(PASSES):
             for j in range(PACK):
                 nc.sync.dma_start(x_sb[a][j][:], xv[a, j])
-        load_gate(0)
         for d in range(D):
             nc.sync.dma_start(pos_sb[d][:], positions[d])
-        load_w(1)
-        load_gate(1)
-        load_w(2)
-        load_gate(2)
-        load_gate(3)
+            nc.sync.dma_start(gate_sb[d][:], gv[d])
 
         ident = keep.tile([P, P], F32, name="ident")
         make_identity(nc, ident[:])
-        b_rows = keep.tile([P, P], F32, name="b_rows")
-        nc.vector.memset(b_rows[:], 0.0)
-        nc.scalar.dma_start(b_rows[0:BLOCKS, :], b.rearrange("(c p) o -> c (p o)", c=BLOCKS))
-        b_ps = psum.tile([P, P], F32, name="b_ps")
-        nc.tensor.transpose(b_ps[:], b_rows[:], ident[:])
-        b_cols = keep.tile([P, BLOCKS], F32, name="b_cols")
-        nc.scalar.copy(b_cols[:], b_ps[:, 0:BLOCKS])
 
-        w_grp = [keep.tile([P, PASSES, nb * P, PACK], BF16, name=f"w_grp{g}", align_bytes=64) for g, (c0, nb) in enumerate(groups)]
-        w_codes = [keep.tile([P, PASSES, nb * P], U32, name=f"w_codes{g}", align_bytes=64) for g, (c0, nb) in enumerate(groups)]
-        w_scales = [keep.tile([P, PASSES, nb * P], U8, name=f"w_scales{g}", align_bytes=64) for g, (c0, nb) in enumerate(groups)]
-
-        def interleave_w(g):
-            for a in range(PASSES):
-                nc.scalar.copy(w_grp[g][:, a, :, :], w_raw[g][:, a, :, :].rearrange("p j n -> p n j"))
-
-        def quantize_w(g):
+        w_grp = [keep.tile([P, N, PACK], BF16, name=f"w_grp{a}", align_bytes=64) for a in range(PASSES)]
+        w_codes = [keep.tile([P, N], U32, name=f"w_codes{a}", align_bytes=64) for a in range(PASSES)]
+        w_scales = [keep.tile([P, N], U8, name=f"w_scales{a}", align_bytes=64) for a in range(PASSES)]
+        for a in range(PASSES):
+            nc.scalar.copy(
+                w_grp[a][:].rearrange("p (c m) j -> p m c j", c=BLOCKS),
+                w_raw[a][:].rearrange("p j (m c) -> p m c j", c=BLOCKS),
+            )
             nc.vector.quantize_mx(
-                out=w_codes[g][:].rearrange("p a n -> p (a n)").bitcast(FP8X4),
-                scales=w_scales[g][:].rearrange("p a n -> p (a n)"),
-                in_=w_grp[g][:].rearrange("p a n j -> p (a n j)"),
+                out=w_codes[a][:].bitcast(FP8X4),
+                scales=w_scales[a][:],
+                in_=w_grp[a][:].rearrange("p n j -> p (n j)"),
             )
 
         x_grp = [keep.tile([P, S, PACK], BF16, name=f"x_grp{a}", align_bytes=64) for a in range(PASSES)]
         x_codes = [keep.tile([P, S], U32, name=f"x_codes{a}", align_bytes=64) for a in range(PASSES)]
         x_scales = [keep.tile([P, S], U8, name=f"x_scales{a}", align_bytes=64) for a in range(PASSES)]
+        y_sb = [keep.tile([P, S], F32, name=f"y_sb{c}") for c in range(BLOCKS)]
 
         def gather_x(a, j, s0, s1):
             nc.vector.tensor_copy(x_grp[a][:, s0:s1, j], x_sb[a][j][:].indirect(offs_sb[:, s0 // 16 : s1 // 16]))
@@ -104,15 +86,11 @@ def tile_picked_sub_lin_relu_sub_e_kernel(tc, xT, w, b, gate, offs, pos1, pos2, 
                 in_=x_grp[a][:, s0:s1, :].rearrange("p s j -> p (s j)"),
             )
 
-        y_sb = [keep.tile([P, S], F32, name=f"y_sb{c}") for c in range(BLOCKS)]
-
         def multiply(acc, c, a, s0, s1):
-            g = min(c, 2)
-            m0 = (c - groups[g][0]) * P
             nc.tensor.matmul_mx(
                 out=acc[:],
-                lhsT=w_codes[g][:, a, m0 : m0 + P].bitcast(FP8X4),
-                lhsT_scale=w_scales[g][:, a, m0 : m0 + P],
+                lhsT=w_codes[a][:, c * P : (c + 1) * P].bitcast(FP8X4),
+                lhsT_scale=w_scales[a][:, c * P : (c + 1) * P],
                 rhs=x_codes[a][:, s0:s1].bitcast(FP8X4),
                 rhs_scale=x_scales[a][:, s0:s1],
                 start=(a == 0),
@@ -122,65 +100,60 @@ def tile_picked_sub_lin_relu_sub_e_kernel(tc, xT, w, b, gate, offs, pos1, pos2, 
         def finish(acc, c, s0, s1):
             nc.scalar.activation(y_sb[c][:, s0:s1], acc[:], RELU, bias=b_cols[:, c : c + 1])
 
-        prods = [[keep.tile([P, V], F32, name=f"prod{c}{d}") for d in range(D)] for c in range(BLOCKS)]
-
-        def neighbour(c, d):
-            nc.vector.tensor_tensor(prods[c][d][:], y_sb[c][:].indirect(pos_sb[d][:]), gate_sb[c][:, d, :], MULT)
-
-        interleave_w(0)
-        quantize_w(0)
         for j in range(PACK):
             gather_x(0, j, 0, S)
         quantize_x(0, 0, S)
-        halves = ((0, HALF), (HALF, S))
-        acc0 = [psum.tile([P, HALF], F32, name=f"acc0{h}") for h in range(2)]
-        for h, (s0, s1) in enumerate(halves):
-            multiply(acc0[h], 0, 0, s0, s1)
+        pieces = [(0, 0, HALF), (0, HALF, S)] + [(c, 0, S) for c in range(1, BLOCKS)]
+        accs = [psum.tile([P, s1 - s0], F32, name=f"acc{i}") for i, (c, s0, s1) in enumerate(pieces)]
+        for acc, (c, s0, s1) in zip(accs, pieces):
+            multiply(acc, c, 0, s0, s1)
         for j in range(PACK - 1):
             gather_x(1, j, 0, S)
-        for s0, s1 in halves:
+        for s0, s1 in ((0, HALF), (HALF, S)):
             gather_x(1, PACK - 1, s0, s1)
-        for h, (s0, s1) in enumerate(halves):
+        for s0, s1 in ((0, HALF), (HALF, S)):
             quantize_x(1, s0, s1)
-            multiply(acc0[h], 0, 1, s0, s1)
-            finish(acc0[h], 0, s0, s1)
+        for acc, (c, s0, s1) in zip(accs, pieces):
+            multiply(acc, c, 1, s0, s1)
+            finish(acc, c, s0, s1)
 
-        def later_block(c):
-            acc = psum.tile([P, S], F32, name="acc", bufs=3)
-            for a in range(PASSES):
-                multiply(acc, c, a, 0, S)
-            finish(acc, c, 0, S)
+        prods = [[keep.tile([P, V], F32, name=f"prod{c}{d}") for d in range(D)] for c in range(BLOCKS)]
 
-        def sums(c):
-            first = work.tile([P, V], F32, name="first")
-            second = work.tile([P, V], F32, name="second")
+        def neighbour(c, d):
+            nc.vector.tensor_tensor(prods[c][d][:], y_sb[c][:].indirect(pos_sb[d][:]), gate_sb[d][:, c, :], MULT)
+
+        def add_up(c, count):
+            banks = [psum.tile([P, P], F32, name=f"sum_t{h}") for h in range(V // P)]
+            for d in range(count):
+                for h in range(V // P):
+                    nc.tensor.matmul(
+                        banks[h][:],
+                        prods[c][d][:, h * P : (h + 1) * P],
+                        ident[:],
+                        start=(d == 0),
+                        stop=(d == count - 1),
+                        is_transpose=True,
+                    )
+            turned = work.tile([P, V], F32, name="turned")
+            for h in range(V // P):
+                nc.scalar.copy(turned[:, h * P : (h + 1) * P], banks[h][:])
+            back = psum.tile([P, V], F32, name="back")
+            for h in range(V // P):
+                nc.tensor.transpose(back[:, h * P : (h + 1) * P], turned[:, h * P : (h + 1) * P], ident[:])
+            return back
+
+        def store(c, total):
+            nc.sync.dma_start(ov[c], total[:])
+
+        for c, d in ((0, 0), (0, 1), (1, 0), (1, 1), (0, 2), (0, 3), (1, 2), (1, 3)):
+            neighbour(c, d)
+        for c in range(BLOCKS):
+            if c >= 2:
+                for d in range(D):
+                    neighbour(c, d)
             total = work.tile([P, V], F32, name="total")
-            nc.vector.tensor_tensor(first[:], prods[c][0][:], prods[c][1][:], ADD)
-            nc.vector.tensor_tensor(second[:], prods[c][2][:], prods[c][3][:], ADD)
-            nc.vector.tensor_tensor(total[:], first[:], second[:], ADD)
-            nc.sync.dma_start(out[c * P : (c + 1) * P, :], total[:])
-
-        interleave_w(1)
-        neighbour(0, 0)
-        neighbour(0, 1)
-        quantize_w(1)
-        later_block(1)
-        interleave_w(2)
-        neighbour(0, 2)
-        neighbour(0, 3)
-        neighbour(1, 0)
-        quantize_w(2)
-        later_block(2)
-        later_block(3)
-        sums(0)
-        for d in range(1, D):
-            neighbour(1, d)
-        neighbour(2, 0)
-        sums(1)
-        for d in range(1, D):
-            neighbour(2, d)
-        neighbour(3, 0)
-        sums(2)
-        for d in range(1, D):
-            neighbour(3, d)
-        sums(3)
+            if c < BLOCKS - 1:
+                nc.scalar.copy(total[:], add_up(c, D)[:])
+            else:
+                nc.vector.tensor_tensor(total[:], prods[c][D - 1][:], add_up(c, D - 1)[:], ADD)
+            store(c, total)

@@ -33,43 +33,58 @@ def tile_picked_sub_lin_relu_sub_e_kernel(tc, xT, w, b, gate, offs, pos1, pos2, 
 
         xv = xT.rearrange("(a p j) t -> a j p t", a=PASSES, j=PACK)
         wv = w.rearrange("(a p j) n -> a p j n", a=PASSES, j=PACK)
-        gv = gate.rearrange("d (p c) v -> d p c v", c=BLOCKS)
-        ov = out.rearrange("(p c) v -> c p v", c=BLOCKS)
+        gv = gate.rearrange("d (c p) v -> c p d v", c=BLOCKS)
+        ov = out.rearrange("(c p) v -> c p v", c=BLOCKS)
 
         offs_sb = lists.tile([P, S // 16], U16, name="offs_sb")
         pos_sb = [lists.tile([P, V // 16], U16, name=f"pos_sb{d}") for d in range(D)]
-        w_raw = [keep.tile([P, PACK, N], F32, name=f"w_raw{a}") for a in range(PASSES)]
+        w_raw = keep.tile([P, PACK, N], F32, name="w_raw")
         x_sb = [[keep.tile([P, T], F32, name=f"x_sb{a}{j}") for j in range(PACK)] for a in range(PASSES)]
-        gate_sb = [keep.tile([P, BLOCKS, V], F32, name=f"gate_sb{d}") for d in range(D)]
+        gate_sb = [keep.tile([P, D, V], F32, name=f"gate_sb{c}") for c in range(BLOCKS)]
         b_cols = keep.tile([P, BLOCKS], F32, name="b_cols")
 
+        b_rows = keep.tile([P, P], F32, name="b_rows")
+        nc.vector.memset(b_rows[:], 0.0)
+        nc.scalar.dma_start(b_rows[0:BLOCKS, :], b.rearrange("(c p) o -> c (p o)", c=BLOCKS))
         nc.sync.dma_start(offs_sb[:], offs)
-        for a in range(PASSES):
-            nc.sync.dma_start(w_raw[a][:], wv[a])
-        nc.scalar.dma_start(b_cols[:], b.rearrange("(p c) o -> p (c o)", c=BLOCKS))
+        nc.sync.dma_start(w_raw[:], wv[0])
         for a in range(PASSES):
             for j in range(PACK):
                 nc.sync.dma_start(x_sb[a][j][:], xv[a, j])
+        w_late = [keep.tile([P, PACK, N // 2], F32, name=f"w_late{h}") for h in range(2)]
+        nc.sync.dma_start(w_late[0][:], wv[1][:, :, 0 : N // 2])
+        nc.sync.dma_start(gate_sb[0][:], gv[0])
         for d in range(D):
             nc.sync.dma_start(pos_sb[d][:], positions[d])
-            nc.sync.dma_start(gate_sb[d][:], gv[d])
+        nc.sync.dma_start(w_late[1][:], wv[1][:, :, N // 2 : N])
+        for c in range(1, BLOCKS):
+            nc.sync.dma_start(gate_sb[c][:], gv[c])
 
         ident = keep.tile([P, P], F32, name="ident")
         make_identity(nc, ident[:])
+        b_turned = psum.tile([P, V], F32, name="back")
+        nc.tensor.transpose(b_turned[:, 0:P], b_rows[:], ident[:])
+        nc.scalar.copy(b_cols[:], b_turned[:, 0:BLOCKS])
+        b_held = keep.tile([P, 1], F32, name="b_held", tag="w_grp1_2", align_bytes=64)
+        nc.scalar.copy(b_held[:], b_turned[:, 1:2])
 
-        w_grp = [keep.tile([P, N, PACK], BF16, name=f"w_grp{a}", align_bytes=64) for a in range(PASSES)]
         w_codes = [keep.tile([P, N], U32, name=f"w_codes{a}", align_bytes=64) for a in range(PASSES)]
         w_scales = [keep.tile([P, N], U8, name=f"w_scales{a}", align_bytes=64) for a in range(PASSES)]
-        for a in range(PASSES):
-            nc.scalar.copy(
-                w_grp[a][:].rearrange("p (c m) j -> p m c j", c=BLOCKS),
-                w_raw[a][:].rearrange("p j (m c) -> p m c j", c=BLOCKS),
-            )
+
+        def interleave_w(grouped, raw, n0):
+            nc.scalar.copy(grouped, raw[:, :, n0 : n0 + P].rearrange("p j m -> p m j"))
+
+        def quantize_w(grouped, a, n0, n1):
             nc.vector.quantize_mx(
-                out=w_codes[a][:].bitcast(FP8X4),
-                scales=w_scales[a][:],
-                in_=w_grp[a][:].rearrange("p n j -> p (n j)"),
+                out=w_codes[a][:, n0:n1].bitcast(FP8X4),
+                scales=w_scales[a][:, n0:n1],
+                in_=grouped.rearrange("p n j -> p (n j)"),
             )
+
+        w_grp0 = keep.tile([P, N, PACK], BF16, name="w_grp0", align_bytes=64)
+        for c in range(BLOCKS):
+            interleave_w(w_grp0[:, c * P : (c + 1) * P, :], w_raw, c * P)
+        quantize_w(w_grp0[:], 0, 0, N)
 
         x_grp = [keep.tile([P, S, PACK], BF16, name=f"x_grp{a}", align_bytes=64) for a in range(PASSES)]
         x_codes = [keep.tile([P, S], U32, name=f"x_codes{a}", align_bytes=64) for a in range(PASSES)]
@@ -98,7 +113,8 @@ def tile_picked_sub_lin_relu_sub_e_kernel(tc, xT, w, b, gate, offs, pos1, pos2, 
             )
 
         def finish(acc, c, s0, s1):
-            nc.scalar.activation(y_sb[c][:, s0:s1], acc[:], RELU, bias=b_cols[:, c : c + 1])
+            bias = b_held[:] if c == 1 else b_cols[:, c : c + 1]
+            nc.scalar.activation(y_sb[c][:, s0:s1], acc[:], RELU, bias=bias)
 
         for j in range(PACK):
             gather_x(0, j, 0, S)
@@ -111,16 +127,28 @@ def tile_picked_sub_lin_relu_sub_e_kernel(tc, xT, w, b, gate, offs, pos1, pos2, 
             gather_x(1, j, 0, S)
         for s0, s1 in ((0, HALF), (HALF, S)):
             gather_x(1, PACK - 1, s0, s1)
-        for s0, s1 in ((0, HALF), (HALF, S)):
-            quantize_x(1, s0, s1)
-        for acc, (c, s0, s1) in zip(accs, pieces):
-            multiply(acc, c, 1, s0, s1)
-            finish(acc, c, s0, s1)
+        def late_weights(c):
+            w_grp1 = keep.tile([P, P, PACK], BF16, name=f"w_grp1_{c}", tag=f"w_grp1_{min(c, 2)}", align_bytes=64)
+            interleave_w(w_grp1[:], w_late[c // 2], (c % 2) * P)
+            quantize_w(w_grp1[:], 1, c * P, (c + 1) * P)
+
+        def close(c):
+            for acc, (block, s0, s1) in zip(accs, pieces):
+                if block == c:
+                    multiply(acc, c, 1, s0, s1)
+                    finish(acc, c, s0, s1)
+
+        quantize_x(1, 0, HALF)
+        late_weights(0)
+        quantize_x(1, HALF, S)
+        close(0)
+        late_weights(1)
+        close(1)
 
         prods = [[keep.tile([P, V], F32, name=f"prod{c}{d}") for d in range(D)] for c in range(BLOCKS)]
 
         def neighbour(c, d):
-            nc.vector.tensor_tensor(prods[c][d][:], y_sb[c][:].indirect(pos_sb[d][:]), gate_sb[d][:, c, :], MULT)
+            nc.vector.tensor_tensor(prods[c][d][:], y_sb[c][:].indirect(pos_sb[d][:]), gate_sb[c][:, d, :], MULT)
 
         def add_up(c, count):
             banks = [psum.tile([P, P], F32, name=f"sum_t{h}") for h in range(V // P)]
@@ -145,15 +173,18 @@ def tile_picked_sub_lin_relu_sub_e_kernel(tc, xT, w, b, gate, offs, pos1, pos2, 
         def store(c, total):
             nc.sync.dma_start(ov[c], total[:])
 
-        for c, d in ((0, 0), (0, 1), (1, 0), (1, 1), (0, 2), (0, 3), (1, 2), (1, 3)):
-            neighbour(c, d)
         for c in range(BLOCKS):
-            if c >= 2:
-                for d in range(D):
-                    neighbour(c, d)
-            total = work.tile([P, V], F32, name="total")
+            for d in range(D):
+                neighbour(c, d)
+            if c + 2 < BLOCKS:
+                late_weights(c + 2)
+                close(c + 2)
+            total = keep.tile([P, V], F32, name=f"total{c}")
             if c < BLOCKS - 1:
                 nc.scalar.copy(total[:], add_up(c, D)[:])
             else:
-                nc.vector.tensor_tensor(total[:], prods[c][D - 1][:], add_up(c, D - 1)[:], ADD)
+                back = add_up(c, 2)
+                pair = keep.tile([P, V], F32, name="pair")
+                nc.vector.tensor_tensor(pair[:], prods[c][2][:], prods[c][3][:], ADD)
+                nc.vector.tensor_tensor(total[:], pair[:], back[:], ADD)
             store(c, total)

@@ -38,8 +38,8 @@ def tile_picked_sub_lin_relu_sub_e_kernel(tc, xT, w, b, gate, offs, pos1, pos2, 
 
         offs_sb = lists.tile([P, S // 16], U16, name="offs_sb")
         pos_sb = [lists.tile([P, V // 16], U16, name=f"pos_sb{d}") for d in range(D)]
-        w_raw = keep.tile([P, PACK, N], F32, name="w_raw")
-        x_sb = [[keep.tile([P, T], F32, name=f"x_sb{a}{j}") for j in range(PACK)] for a in range(PASSES)]
+        w_raw = [keep.tile([P, PACK, N], F32, name=f"w_raw{a}") for a in range(PASSES)]
+        x_sb = [[keep.tile([P, T], F32, name=f"x_sb{a}{j}", tag=f"x_sb{a}{j}", align_bytes=64) for j in range(PACK)] for a in range(PASSES)]
         gate_sb = [keep.tile([P, D, V], F32, name=f"gate_sb{c}") for c in range(BLOCKS)]
         b_cols = keep.tile([P, BLOCKS], F32, name="b_cols")
 
@@ -47,16 +47,14 @@ def tile_picked_sub_lin_relu_sub_e_kernel(tc, xT, w, b, gate, offs, pos1, pos2, 
         nc.vector.memset(b_rows[:], 0.0)
         nc.scalar.dma_start(b_rows[0:BLOCKS, :], b.rearrange("(c p) o -> c (p o)", c=BLOCKS))
         nc.sync.dma_start(offs_sb[:], offs)
-        nc.sync.dma_start(w_raw[:], wv[0])
+        nc.sync.dma_start(w_raw[0][:], wv[0])
         for a in range(PASSES):
             for j in range(PACK):
                 nc.sync.dma_start(x_sb[a][j][:], xv[a, j])
-        w_late = [keep.tile([P, PACK, N // 2], F32, name=f"w_late{h}") for h in range(2)]
-        nc.sync.dma_start(w_late[0][:], wv[1][:, :, 0 : N // 2])
+        nc.sync.dma_start(w_raw[1][:], wv[1])
         nc.sync.dma_start(gate_sb[0][:], gv[0])
         for d in range(D):
             nc.sync.dma_start(pos_sb[d][:], positions[d])
-        nc.sync.dma_start(w_late[1][:], wv[1][:, :, N // 2 : N])
         for c in range(1, BLOCKS):
             nc.sync.dma_start(gate_sb[c][:], gv[c])
 
@@ -65,14 +63,14 @@ def tile_picked_sub_lin_relu_sub_e_kernel(tc, xT, w, b, gate, offs, pos1, pos2, 
         b_turned = psum.tile([P, V], F32, name="back")
         nc.tensor.transpose(b_turned[:, 0:P], b_rows[:], ident[:])
         nc.scalar.copy(b_cols[:], b_turned[:, 0:BLOCKS])
-        b_held = keep.tile([P, 1], F32, name="b_held", tag="w_grp1_2", align_bytes=64)
-        nc.scalar.copy(b_held[:], b_turned[:, 1:2])
+        b_held = keep.tile([P, 1], F32, name="b_held", tag="w_grp_last", align_bytes=64)
+        nc.scalar.copy(b_held[:], b_turned[:, 0:1])
 
         w_codes = [keep.tile([P, N], U32, name=f"w_codes{a}", align_bytes=64) for a in range(PASSES)]
         w_scales = [keep.tile([P, N], U8, name=f"w_scales{a}", align_bytes=64) for a in range(PASSES)]
 
-        def interleave_w(grouped, raw, n0):
-            nc.scalar.copy(grouped, raw[:, :, n0 : n0 + P].rearrange("p j m -> p m j"))
+        def interleave_w(copy, grouped, a, c):
+            copy(grouped, w_raw[a][:, :, c * P : (c + 1) * P].rearrange("p j m -> p m j"))
 
         def quantize_w(grouped, a, n0, n1):
             nc.vector.quantize_mx(
@@ -83,7 +81,7 @@ def tile_picked_sub_lin_relu_sub_e_kernel(tc, xT, w, b, gate, offs, pos1, pos2, 
 
         w_grp0 = keep.tile([P, N, PACK], BF16, name="w_grp0", align_bytes=64)
         for c in range(BLOCKS):
-            interleave_w(w_grp0[:, c * P : (c + 1) * P, :], w_raw, c * P)
+            interleave_w(nc.scalar.copy, w_grp0[:, c * P : (c + 1) * P, :], 0, c)
         quantize_w(w_grp0[:], 0, 0, N)
 
         x_grp = [keep.tile([P, S, PACK], BF16, name=f"x_grp{a}", align_bytes=64) for a in range(PASSES)]
@@ -113,7 +111,7 @@ def tile_picked_sub_lin_relu_sub_e_kernel(tc, xT, w, b, gate, offs, pos1, pos2, 
             )
 
         def finish(acc, c, s0, s1):
-            bias = b_held[:] if c == 1 else b_cols[:, c : c + 1]
+            bias = b_held[:] if c == 0 else b_cols[:, c : c + 1]
             nc.scalar.activation(y_sb[c][:, s0:s1], acc[:], RELU, bias=bias)
 
         for j in range(PACK):
@@ -123,14 +121,13 @@ def tile_picked_sub_lin_relu_sub_e_kernel(tc, xT, w, b, gate, offs, pos1, pos2, 
         accs = [psum.tile([P, s1 - s0], F32, name=f"acc{i}") for i, (c, s0, s1) in enumerate(pieces)]
         for acc, (c, s0, s1) in zip(accs, pieces):
             multiply(acc, c, 0, s0, s1)
-        for j in range(PACK - 1):
+        for j in range(PACK):
             gather_x(1, j, 0, S)
-        for s0, s1 in ((0, HALF), (HALF, S)):
-            gather_x(1, PACK - 1, s0, s1)
-        def late_weights(c):
-            w_grp1 = keep.tile([P, P, PACK], BF16, name=f"w_grp1_{c}", tag=f"w_grp1_{min(c, 2)}", align_bytes=64)
-            interleave_w(w_grp1[:], w_late[c // 2], (c % 2) * P)
-            quantize_w(w_grp1[:], 1, c * P, (c + 1) * P)
+        quantize_x(1, 0, S)
+
+        def late_weights(c, grouped):
+            interleave_w(nc.vector.tensor_copy if c == 0 else nc.scalar.copy, grouped, 1, c)
+            quantize_w(grouped, 1, c * P, (c + 1) * P)
 
         def close(c):
             for acc, (block, s0, s1) in zip(accs, pieces):
@@ -138,11 +135,10 @@ def tile_picked_sub_lin_relu_sub_e_kernel(tc, xT, w, b, gate, offs, pos1, pos2, 
                     multiply(acc, c, 1, s0, s1)
                     finish(acc, c, s0, s1)
 
-        quantize_x(1, 0, HALF)
-        late_weights(0)
-        quantize_x(1, HALF, S)
+        w_grp1 = keep.tile([P, 2 * P, PACK], BF16, name="w_grp1", tag="x_sb13", align_bytes=64)
+        late_weights(0, w_grp1[:, 0:P, :])
         close(0)
-        late_weights(1)
+        late_weights(1, w_grp1[:, P : 2 * P, :])
         close(1)
 
         prods = [[keep.tile([P, V], F32, name=f"prod{c}{d}") for d in range(D)] for c in range(BLOCKS)]
@@ -173,12 +169,13 @@ def tile_picked_sub_lin_relu_sub_e_kernel(tc, xT, w, b, gate, offs, pos1, pos2, 
         def store(c, total):
             nc.sync.dma_start(ov[c], total[:])
 
+        w_grp_last = keep.tile([P, 2 * P, PACK], BF16, name="w_grp_last", tag="w_grp_last", align_bytes=64)
         for c in range(BLOCKS):
             for d in range(D):
                 neighbour(c, d)
-            if c + 2 < BLOCKS:
-                late_weights(c + 2)
-                close(c + 2)
+                if c == 0 and d in (1, 2):
+                    late_weights(d + 1, w_grp_last[:, (d - 1) * P : d * P, :])
+                    close(d + 1)
             total = keep.tile([P, V], F32, name=f"total{c}")
             if c < BLOCKS - 1:
                 nc.scalar.copy(total[:], add_up(c, D)[:])

from contextlib import ExitStack

import concourse.mybir as mybir
from concourse.masks import make_identity

F32 = mybir.dt.float32
BF16 = mybir.dt.bfloat16
U32 = mybir.dt.uint32
U16 = mybir.dt.uint16
U8 = mybir.dt.uint8
FP8X4 = mybir.dt.float8_e4m3fn_x4
MULT = mybir.AluOpType.mult
ADD = mybir.AluOpType.add
RELU = mybir.ActivationFunctionType.Relu

K, T, D, S, V, N = 1024, 2048, 4, 512, 256, 512
P = 128
PACK = 4
PASSES = K // (P * PACK)
BLOCKS = N // P
HALF = S // 2
FLOPS = 2 * N * K * S


def tile_picked_sub_lin_relu_sub_e_kernel(tc, xT, w, b, gate, offs, pos1, pos2, pos3, pos4, out):
    nc = tc.nc
    positions = (pos1, pos2, pos3, pos4)
    with ExitStack() as ctx:
        lists = ctx.enter_context(tc.tile_pool(name="lists", bufs=1))
        keep = ctx.enter_context(tc.tile_pool(name="keep", bufs=1))
        work = ctx.enter_context(tc.tile_pool(name="work", bufs=2))
        psum = ctx.enter_context(tc.psum_pool(name="psum", bufs=1))

        xv = xT.rearrange("(a p j) t -> a j p t", a=PASSES, j=PACK)
        wv = w.rearrange("(a p j) n -> a p j n", a=PASSES, j=PACK)
        gv = gate.rearrange("d (c p) v -> c p d v", c=BLOCKS)
        ov = out.rearrange("(c p) v -> c p v", c=BLOCKS)

        offs_sb = lists.tile([P, S // 16], U16, name="offs_sb")
        pos_sb = [lists.tile([P, V // 16], U16, name=f"pos_sb{d}") for d in range(D)]
        w_raw = [keep.tile([P, PACK, N], F32, name=f"w_raw{a}") for a in range(PASSES)]
        x_sb = [[keep.tile([P, T], F32, name=f"x_sb{a}{j}", tag=f"x_sb{a}{j}", align_bytes=64) for j in range(PACK)] for a in range(PASSES)]
        gate_sb = [keep.tile([P, D, V], F32, name=f"gate_sb{c}") for c in range(BLOCKS)]
        b_cols = keep.tile([P, BLOCKS], F32, name="b_cols")

        b_rows = keep.tile([P, P], F32, name="b_rows")
        nc.vector.memset(b_rows[:], 0.0)
        nc.scalar.dma_start(b_rows[0:BLOCKS, :], b.rearrange("(c p) o -> c (p o)", c=BLOCKS))
        nc.sync.dma_start(offs_sb[:], offs)
        nc.sync.dma_start(w_raw[0][:], wv[0])
        for a in range(PASSES):
            for j in range(PACK):
                nc.sync.dma_start(x_sb[a][j][:], xv[a, j])
        nc.sync.dma_start(w_raw[1][:], wv[1])
        nc.sync.dma_start(gate_sb[0][:], gv[0])
        for d in range(D):
            nc.sync.dma_start(pos_sb[d][:], positions[d])
        for c in range(1, BLOCKS):
            nc.sync.dma_start(gate_sb[c][:], gv[c])

        ident = keep.tile([P, P], F32, name="ident")
        make_identity(nc, ident[:])
        b_turned = psum.tile([P, V], F32, name="back")
        nc.tensor.transpose(b_turned[:, 0:P], b_rows[:], ident[:])
        nc.scalar.copy(b_cols[:], b_turned[:, 0:BLOCKS])
        b_held = keep.tile([P, 1], F32, name="b_held", tag="w_grp_last", align_bytes=64)
        nc.scalar.copy(b_held[:], b_turned[:, 0:1])

        w_codes = [keep.tile([P, N], U32, name=f"w_codes{a}", align_bytes=64) for a in range(PASSES)]
        w_scales = [keep.tile([P, N], U8, name=f"w_scales{a}", align_bytes=64) for a in range(PASSES)]

        def interleave_w(copy, grouped, a, c):
            copy(grouped, w_raw[a][:, :, c * P : (c + 1) * P].rearrange("p j m -> p m j"))

        def quantize_w(grouped, a, n0, n1):
            nc.vector.quantize_mx(
                out=w_codes[a][:, n0:n1].bitcast(FP8X4),
                scales=w_scales[a][:, n0:n1],
                in_=grouped.rearrange("p n j -> p (n j)"),
            )

        w_grp0 = keep.tile([P, N, PACK], BF16, name="w_grp0", align_bytes=64)
        for c in range(BLOCKS):
            interleave_w(nc.scalar.copy, w_grp0[:, c * P : (c + 1) * P, :], 0, c)
        quantize_w(w_grp0[:], 0, 0, N)

        x_grp = [keep.tile([P, S, PACK], BF16, name=f"x_grp{a}", align_bytes=64) for a in range(PASSES)]
        x_codes = [keep.tile([P, S], U32, name=f"x_codes{a}", align_bytes=64) for a in range(PASSES)]
        x_scales = [keep.tile([P, S], U8, name=f"x_scales{a}", align_bytes=64) for a in range(PASSES)]
        y_sb = [keep.tile([P, S], F32, name=f"y_sb{c}") for c in range(BLOCKS)]

        def gather_x(a, j, s0, s1):
            nc.vector.tensor_copy(x_grp[a][:, s0:s1, j], x_sb[a][j][:].indirect(offs_sb[:, s0 // 16 : s1 // 16]))

        def quantize_x(a, s0, s1):
            nc.vector.quantize_mx(
                out=x_codes[a][:, s0:s1].bitcast(FP8X4),
                scales=x_scales[a][:, s0:s1],
                in_=x_grp[a][:, s0:s1, :].rearrange("p s j -> p (s j)"),
            )

        def multiply(acc, c, a, s0, s1):
            nc.tensor.matmul_mx(
                out=acc[:],
                lhsT=w_codes[a][:, c * P : (c + 1) * P].bitcast(FP8X4),
                lhsT_scale=w_scales[a][:, c * P : (c + 1) * P],
                rhs=x_codes[a][:, s0:s1].bitcast(FP8X4),
                rhs_scale=x_scales[a][:, s0:s1],
                start=(a == 0),
                stop=(a == PASSES - 1),
            )

        def finish(acc, c, s0, s1):
            bias = b_held[:] if c == 0 else b_cols[:, c : c + 1]
            nc.scalar.activation(y_sb[c][:, s0:s1], acc[:], RELU, bias=bias)

        for j in range(PACK):
            gather_x(0, j, 0, S)
        quantize_x(0, 0, S)
        pieces = [(0, 0, HALF), (0, HALF, S)] + [(c, 0, S) for c in range(1, BLOCKS)]
        accs = [psum.tile([P, s1 - s0], F32, name=f"acc{i}") for i, (c, s0, s1) in enumerate(pieces)]
        for acc, (c, s0, s1) in zip(accs, pieces):
            multiply(acc, c, 0, s0, s1)
        for j in range(PACK):
            gather_x(1, j, 0, S)
        quantize_x(1, 0, S)

        def late_weights(c, grouped):
            interleave_w(nc.vector.tensor_copy if c == 0 else nc.scalar.copy, grouped, 1, c)
            quantize_w(grouped, 1, c * P, (c + 1) * P)

        def close(c):
            for acc, (block, s0, s1) in zip(accs, pieces):
                if block == c:
                    multiply(acc, c, 1, s0, s1)
                    finish(acc, c, s0, s1)

        w_grp1 = keep.tile([P, 2 * P, PACK], BF16, name="w_grp1", tag="x_sb13", align_bytes=64)
        late_weights(0, w_grp1[:, 0:P, :])
        close(0)
        late_weights(1, w_grp1[:, P : 2 * P, :])
        close(1)

        prods = [[keep.tile([P, V], F32, name=f"prod{c}{d}") for d in range(D)] for c in range(BLOCKS)]

        def neighbour(c, d):
            nc.vector.tensor_tensor(prods[c][d][:], y_sb[c][:].indirect(pos_sb[d][:]), gate_sb[c][:, d, :], MULT)

        def add_up(c, count):
            banks = [psum.tile([P, P], F32, name=f"sum_t{h}") for h in range(V // P)]
            for d in range(count):
                for h in range(V // P):
                    nc.tensor.matmul(
                        banks[h][:],
                        prods[c][d][:, h * P : (h + 1) * P],
                        ident[:],
                        start=(d == 0),
                        stop=(d == count - 1),
                        is_transpose=True,
                    )
            turned = work.tile([P, V], F32, name="turned")
            for h in range(V // P):
                nc.scalar.copy(turned[:, h * P : (h + 1) * P], banks[h][:])
            back = psum.tile([P, V], F32, name="back")
            for h in range(V // P):
                nc.tensor.transpose(back[:, h * P : (h + 1) * P], turned[:, h * P : (h + 1) * P], ident[:])
            return back

        def store(c, total):
            nc.sync.dma_start(ov[c], total[:])

        w_grp_last = keep.tile([P, 2 * P, PACK], BF16, name="w_grp_last", tag="w_grp_last", align_bytes=64)
        for c in range(BLOCKS):
            for d in range(D):
                neighbour(c, d)
                if c == 0 and d in (1, 2):
                    late_weights(d + 1, w_grp_last[:, (d - 1) * P : d * P, :])
                    close(d + 1)
            total = keep.tile([P, V], F32, name=f"total{c}")
            if c < BLOCKS - 1:
                nc.scalar.copy(total[:], add_up(c, D)[:])
            else:
                back = add_up(c, 2)
                pair = keep.tile([P, V], F32, name="pair")
                nc.vector.tensor_tensor(pair[:], prods[c][2][:], prods[c][3][:], ADD)
                nc.vector.tensor_tensor(total[:], pair[:], back[:], ADD)
            store(c, total)
